import numpy as np
import ml_dtypes


def mxq(x, axis, fmt="e4m3"):
    dtype, down = {"e4m3": (ml_dtypes.float8_e4m3fn, 7), "e5m2": (ml_dtypes.float8_e5m2, 14)}[fmt]
    v = np.moveaxis(np.asarray(x, np.float32).astype(ml_dtypes.bfloat16).astype(np.float64), axis, -1)
    blocks = v.reshape(v.shape[:-1] + (-1, 32))
    amax = np.abs(blocks).max(-1, keepdims=True)
    byte = np.maximum(np.where(amax > 0, np.frexp(amax)[1] - 1 + 127, 0) - down, 1)
    scale = np.exp2(byte - 127.0)
    codes = (blocks / scale).astype(np.float32).astype(dtype).astype(np.float64)
    return np.moveaxis((codes * scale).reshape(v.shape), -1, axis)


WIDE = False


def mx_kscale(k):
    if not WIDE:
        return np.ones(k)
    levels = np.array([10, -10, 5, -5, 0])
    if k % 512:
        return np.exp2(np.random.permutation(np.resize(levels, k // 32))).repeat(32)
    a = np.empty((k // 512, 16))
    for p in range(k // 512):
        a[p, :8] = np.random.permutation(np.resize(levels, 8))
        for g in range(8):
            far = levels[np.abs(levels - a[p, g]) >= 10]
            a[p, g + 8] = far[np.random.randint(len(far))]
    return np.exp2(a.ravel()).repeat(32)


BF16 = ml_dtypes.bfloat16


def bf(x):
    return np.asarray(x, np.float32).astype(BF16)


def f64(x):
    return np.asarray(x).astype(np.float64)


E2M1 = np.array([0.0, 0.5, 1.0, 1.5, 2.0, 3.0, 4.0, 6.0, -0.0, -0.5, -1.0, -1.5, -2.0, -3.0, -4.0, -6.0])


def pack_weight(w, fmt):
    k, n = w.shape
    w = f64(bf(w)).reshape(k // 32, 32, n)
    amax = np.abs(w).max(1)
    if fmt == "e4m3":
        byte = np.frexp(amax)[1] - 1 + 127 - 7
    else:
        mant, ex = np.frexp(amax / 6.0)
        byte = np.where(mant > 0.5, ex, ex - 1) + 127
    byte = np.clip(np.where(amax > 0, byte, 1), 1, 254)
    scaled = (w * np.exp2(127.0 - byte)[:, None, :]).reshape(k, n).astype(np.float32)
    by_word = np.ascontiguousarray(scaled.reshape(k // 512, 128, 4, n).transpose(0, 1, 3, 2))
    if fmt == "e4m3":
        words = by_word.astype(ml_dtypes.float8_e4m3fn).view(np.uint8)
    else:
        c = by_word.astype(ml_dtypes.float4_e2m1fn).view(np.uint8) & 0xF
        words = c[..., 0::2] | (c[..., 1::2] << 4)
    return np.ascontiguousarray(words), np.ascontiguousarray(byte.astype(np.uint8).reshape(k // 512, 16, n))


def unpack_weight(words, scales, fmt):
    g, p, n, _ = words.shape
    if fmt == "e4m3":
        vals = np.ascontiguousarray(words).view(ml_dtypes.float8_e4m3fn).astype(np.float64)
    else:
        nib = np.empty((g, p, n, 4), np.uint8)
        nib[..., 0::2] = words & 0xF
        nib[..., 1::2] = words >> 4
        vals = E2M1[nib]
    vals = vals * np.repeat(np.exp2(scales.astype(np.float64) - 127.0), 8, axis=1)[..., None]
    return vals.transpose(0, 1, 3, 2).reshape(g * 512, n)
def pack4(w):
    words, scales = pack_weight(w, "e2m1")
    return words.reshape(words.shape[0], 128, -1), scales


def unpack4(words, scales):
    return unpack_weight(words.reshape(words.shape[0], 128, -1, 2), scales, "e2m1")


E4M3FN = np.array([(-1.0 if i & 128 else 1.0) * ((1.0 + (i & 7) / 8.0) * 2.0 ** (((i >> 3) & 15) - 7) if i & 120 else (i & 7) * 2.0 ** -9) for i in range(256)])


def e4m3fn_bytes(y):
    return np.clip(np.asarray(y, np.float64), -448.0, 448.0).astype(np.float32).astype(ml_dtypes.float8_e4m3fn).view(np.uint8)


def e4m3fn_values(b):
    return E4M3FN[b]


T, N, M, R, B = 1024, 2048, 1024, 512, 128


def setup_inputs():
    s, t = mx_kscale(M), mx_kscale(N)
    x = np.random.standard_normal((T, M)) * M ** 0.25
    y = np.random.standard_normal((N, M)) * M ** 0.25
    x = (x - x.mean(1, keepdims=True)) * s
    y = (y - y.mean(1, keepdims=True)) / s
    x_scale = (np.abs(x).reshape(T, M // B, B).max(2) / 448).astype(np.float32)
    y_scale = (np.abs(y).reshape(N // B, B, M // B, B).max((1, 3)) / 448).astype(np.float32)
    x_bytes = e4m3fn_bytes(x / np.repeat(f64(x_scale), B, 1))
    y_bytes = e4m3fn_bytes(y / np.repeat(np.repeat(f64(y_scale), B, 0), B, 1))
    a, b = 2 * np.random.random(T), 2 * np.random.random(N)
    rho = np.exp(-np.abs(a[:, None] - b)) * t
    h_words, h_scales = pack4(np.random.standard_normal((N, R)) / np.sqrt(N) / t[:, None])
    return {"x_bytes": x_bytes, "x_scale": x_scale, "y_bytes": y_bytes, "y_scale": y_scale,
            "rho": bf(rho), "h_words": h_words, "h_scales": h_scales}


def reference(x_bytes, x_scale, y_bytes, y_scale, rho, h_words, h_scales):
    x = e4m3fn_values(x_bytes) * np.repeat(f64(x_scale), B, 1)
    y = e4m3fn_values(y_bytes) * np.repeat(np.repeat(f64(y_scale), B, 0), B, 1)
    c = (mxq(x, 1, "e4m3") @ mxq(y, 1, "e4m3").T) / (M - 1)
    z = c * f64(rho)
    return mxq(z, 1, "e4m3") @ unpack4(h_words, h_scales)

@@ -1,0 +1,272 @@
+from contextlib import ExitStack
+
+import concourse.mybir as mybir
+from concourse.masks import make_identity
+
+T, N, M, R = 1024, 2048, 1024, 512
+P = 128
+FLOPS = 2 * T * N * M + 2 * T * N * R
+
+F32 = mybir.dt.float32
+BF16 = mybir.dt.bfloat16
+I32 = mybir.dt.int32
+U32 = mybir.dt.uint32
+U8 = mybir.dt.uint8
+FP8 = mybir.dt.float8_e4m3fn
+FP8X4 = mybir.dt.float8_e4m3fn_x4
+FP4X4 = mybir.dt.float4_e2m1fn_x4
+MULT = mybir.AluOpType.mult
+COPY = mybir.ActivationFunctionType.Copy
+
+PREPS = [("y", 0), ("y", 1), ("x", 0), ("x", 1), ("x", 2), ("y", 2), ("y", 3), ("y", 4), ("y", 5), ("y", 6), ("y", 7), ("x", 3)]
+SLOTS = [
+    (0, None), (1, None), (2, None), (3, (0, 0)), (4, (1, 0)), (5, (2, 0)), (6, None), (7, (0, 1)), (8, (1, 1)), (None, (2, 1)), (9, (0, 2)), (10, (1, 2)), (None, (2, 2)), (11, (0, 3)), (None, (1, 3)), (None, (2, 3)), (None, (3, 0)), (None, (3, 1)), (None, (3, 2)), (None, (3, 3)),
+]
+
+
+def tile_localised_ensemble_covariance_d4_kernel(tc, x_bytes, x_scale, y_bytes, y_scale, rho, h_words, h_scales, out):
+    nc = tc.nc
+    with ExitStack() as ctx:
+        keep = ctx.enter_context(tc.tile_pool(name="keep", bufs=1))
+        wide_pool = ctx.enter_context(tc.tile_pool(name="wide", bufs=6))
+        stage = ctx.enter_context(tc.tile_pool(name="stage", bufs=3))
+        psum_t = ctx.enter_context(tc.psum_pool(name="psum_t", bufs=4))
+        psum_a = ctx.enter_context(tc.psum_pool(name="psum_a", bufs=4))
+        ctx.enter_context(tc.manual_schedule())
+
+        ysc = keep.tile([P, 16, 8], F32, name="ysc")
+        nc.scalar.dma_start(out=ysc[:].rearrange("p b k -> p (b k)"), in_=y_scale.rearrange("b k -> (b k)").partition_broadcast(P))
+        xsc = keep.tile([P, 8, 8], F32, name="xsc")
+        nc.scalar.dma_start(out=xsc[:], in_=x_scale.rearrange("(i p) k -> p i k", p=P))
+
+        src = {"x": x_bytes.rearrange("(u p) k -> p u k", p=P), "y": y_bytes.rearrange("(u p) k -> p u k", p=P)}
+        raw = {}
+        rho_rows = rho.rearrange("(i p) n -> p i n", p=P)
+        rho_t = {}
+
+        def load(kind, j):
+            t = keep.tile([P, 2, M], U8, name=f"raw_{kind}{j}")
+            if (kind, j) == ("y", 0):
+                for a in range(2):
+                    nc.sync.dma_start(out=t[:, a, :], in_=src[kind][:, 2 * j + a, :])
+            else:
+                nc.sync.dma_start(out=t[:], in_=src[kind][:, 2 * j : 2 * j + 2, :])
+            raw[kind, j] = t
+
+        def load_rho(q, g):
+            t = keep.tile([P, 2, 512], BF16, name=f"rho_{q}_{g}")
+            nc.sync.dma_start(out=t[:], in_=rho_rows[:, 2 * q : 2 * q + 2, 512 * g : 512 * g + 512])
+            rho_t[q, g] = t
+
+        for pi, zp in SLOTS:
+            if pi is not None:
+                load(*PREPS[pi])
+            if zp is not None:
+                load_rho(*zp)
+        hw = keep.tile([P, 4, 2 * R], U8, name="hw", align_bytes=64)
+        nc.sync.dma_start(out=hw[:].bitcast(I32), in_=h_words.rearrange("g p c -> p g c").bitcast(I32))
+        hs = keep.tile([P, 4, R], U8, name="hs", align_bytes=64)
+        nc.gpsimd.memset(hs[:].bitcast(I32), 0)
+        for quad in range(4):
+            nc.sync.dma_start(
+                out=hs[32 * quad : 32 * quad + 4, :, :].bitcast(I32),
+                in_=h_scales[:, 4 * quad : 4 * quad + 4, :].rearrange("g q n -> q g n").bitcast(I32),
+            )
+
+        ident = keep.tile([P, P], F32, name="ident")
+        make_identity(nc, ident[:])
+
+        codes = {}
+        scales = {}
+        for g in range(4):
+            codes["y", g] = keep.tile([P, 2, 512], U32, name=f"yq{g}", align_bytes=64)
+            scales["y", g] = keep.tile([P, 2, 512], U8, name=f"ys{g}", align_bytes=64)
+        for q in range(4):
+            codes["x", q] = keep.tile([P, 2, 256], U32, name=f"xq{q}", align_bytes=64)
+            scales["x", q] = keep.tile([P, 2, 256], U8, name=f"xs{q}", align_bytes=64)
+            for g in range(4):
+                codes["z", q, g] = keep.tile([P, 256], U32, name=f"zq{q}{g}", align_bytes=64)
+                scales["z", q, g] = keep.tile([P, 256], U8, name=f"zs{q}{g}", align_bytes=64)
+
+        widened = {}
+
+        def on_vector(pi, a, g):
+            return g == 0 or (pi == 0 and a == 0) or (pi in (1, 2))
+
+        def widen(pi, engine):
+            kind, j = PREPS[pi]
+            for a in range(2):
+                if (pi, a) not in widened:
+                    widened[pi, a] = wide_pool.tile([P, 2, 512], BF16, name="wide", align_bytes=64)
+                w = widened[pi, a]
+                for g in range(2):
+                    if on_vector(pi, a, g) != (engine == "v"):
+                        continue
+                    for b in range(4):
+                        k0 = 512 * g + 128 * b
+                        src_ap = raw[kind, j][:, a, k0 : k0 + 128].bitcast(FP8)
+                        sc = ysc if kind == "y" else xsc
+                        s_ap = sc[:, 2 * j + a, 4 * g + b : 4 * g + b + 1]
+                        if engine == "v":
+                            dst = w[:, g, :].rearrange("p (u q e) -> p q u e", u=2, e=2)[:, 32 * b : 32 * b + 32, :, :]
+                            nc.vector.tensor_scalar(out=dst, in0=src_ap.rearrange("p (q u e) -> p q u e", u=2, e=2), scalar1=s_ap, scalar2=None, op0=MULT)
+                        else:
+                            nc.scalar.activation(out=w[:, g, 128 * b : 128 * b + 128], in_=src_ap, func=COPY, scale=s_ap)
+
+        grouped = {}
+
+        def turn_prep(pi):
+            banks = []
+            for a in range(2):
+                bank = psum_t.tile([P, 2, 2, P], F32, name="turn")
+                words = widened[pi, a][:].bitcast(F32)
+                for g in range(2):
+                    for u in range(2):
+                        if on_vector(pi, a, g):
+                            s = words[:, g, 128 * u : 128 * u + 128]
+                        else:
+                            s = words[:, g, u : 256 : 2]
+                        nc.tensor.transpose(bank[:, g, u, :], s, ident[:])
+                banks.append(bank)
+            return banks
+
+        def empty_prep(pi, banks):
+            t = stage.tile([P, 2, 2, P, 4], BF16, name="grouped", align_bytes=64)
+            for a in range(2):
+                nc.scalar.copy(
+                    out=t[:, :, a, :, :].bitcast(F32),
+                    in_=banks[a][:].rearrange("p g u r -> p g r u"),
+                )
+            grouped[pi] = t
+
+        def quant_prep(pi):
+            kind, j = PREPS[pi]
+            key, c0 = (("y", j // 2), 256 * (j % 2)) if kind == "y" else (("x", j), 0)
+            for g in range(2):
+                nc.vector.quantize_mx(
+                    out=codes[key][:, g, c0 : c0 + 256].bitcast(FP8X4),
+                    scales=scales[key][:, g, c0 : c0 + 256],
+                    in_=grouped[pi][:, g, :, :, :].rearrange("p a r j -> p (a r j)"),
+                )
+
+        def first_product(q, g):
+            banks = []
+            for a in range(2):
+                acc = psum_a.tile([P, 512], F32, name="acc")
+                for k in range(2):
+                    nc.tensor.matmul_mx(
+                        out=acc[:],
+                        lhsT=codes["x", q][:, k, 128 * a : 128 * a + 128].bitcast(FP8X4),
+                        lhsT_scale=scales["x", q][:, k, 128 * a : 128 * a + 128],
+                        rhs=codes["y", g][:, k, :].bitcast(FP8X4),
+                        rhs_scale=scales["y", g][:, k, :],
+                        start=(k == 0),
+                        stop=(k == 1),
+                    )
+                banks.append(acc)
+            return banks
+
+        def localise(q, g, banks):
+            zs = []
+            for a in range(2):
+                z = stage.tile([P, 2, 256], BF16, name=f"z{a}", align_bytes=64)
+                for u in range(2):
+                    nc.vector.scalar_tensor_tensor(
+                        out=z[:, u, :].rearrange("p (q e) -> p q e", e=2),
+                        in0=banks[a][:].rearrange("p (q u e) -> p u q e", u=2, e=2)[:, u, :, :],
+                        scalar=1.0 / (M - 1),
+                        in1=rho_t[q, g][:, a, :].rearrange("p (q u e) -> p u q e", u=2, e=2)[:, u, :, :],
+                        op0=MULT,
+                        op1=MULT,
+                    )
+                zs.append(z)
+            return zs
+
+        def turn_z(zs):
+            bank = psum_t.tile([P, 2, 2, P], F32, name="turn")
+            for a in range(2):
+                words = zs[a][:].bitcast(F32)
+                for u in range(2):
+                    nc.tensor.transpose(bank[:, a, u, :], words[:, u, :], ident[:])
+            return bank
+
+        def empty_z(bank):
+            t = stage.tile([P, 2, P, 4], BF16, name="zgrouped", align_bytes=64)
+            nc.scalar.copy(out=t[:].bitcast(F32), in_=bank[:].rearrange("p a u r -> p a r u"))
+            return t
+
+        def quant_z(q, g, t):
+            nc.vector.quantize_mx(
+                out=codes["z", q, g][:].bitcast(FP8X4),
+                scales=scales["z", q, g][:],
+                in_=t[:].rearrange("p a r j -> p (a r j)"),
+            )
+
+        def second_product(i):
+            acc = psum_a.tile([P, 512], F32, name="acc")
+            q, a = divmod(i, 2)
+            for g in range(4):
+                nc.tensor.matmul_mx(
+                    out=acc[:],
+                    lhsT=codes["z", q, g][:, 128 * a : 128 * a + 128].bitcast(FP8X4),
+                    lhsT_scale=scales["z", q, g][:, 128 * a : 128 * a + 128],
+                    rhs=hw[:, g, :].bitcast(FP4X4),
+                    rhs_scale=hs[:, g, :],
+                    start=(g == 0),
+                    stop=(g == 3),
+                )
+            return acc
+
+        def store(i, acc):
+            o = stage.tile([P, R], F32, name="o")
+            nc.scalar.copy(out=o[:], in_=acc[:])
+            nc.sync.dma_start(out=out[128 * i : 128 * i + 128, :], in_=o[:])
+
+        order = list(SLOTS) + [(None, None)] * (2 + 1)
+        widen(0, "v")
+        widen(0, "s")
+        turned = None
+        z_mult = []
+        z_turned = None
+        todo = []
+        done = []
+        for s, (pi, zp) in enumerate(order):
+            nxt = order[s + 1][0] if s + 1 < len(order) else None
+            if nxt is not None:
+                widen(nxt, "v")
+                widen(nxt, "s")
+            if turned is not None:
+                quant_prep(turned)
+                turned = None
+            if z_turned is not None:
+                quant_z(*z_turned)
+                if z_turned[1] == 3:
+                    todo.extend([2 * z_turned[0], 2 * z_turned[0] + 1])
+                z_turned = None
+            z_now = None
+            if z_mult and (z_mult[0][0] <= s - 2 or (s >= len(SLOTS))):
+                z_now = z_mult.pop(0)[1]
+            if pi is not None:
+                banks = turn_prep(pi)
+            if z_now is not None:
+                zbank = turn_z(z_now[2])
+            if pi is not None:
+                empty_prep(pi, banks)
+                turned = pi
+            if z_now is not None:
+                z_turned = (z_now[0], z_now[1], empty_z(zbank))
+            for i, acc in done:
+                store(i, acc)
+            done = []
+            if zp is not None:
+                cbanks = first_product(*zp)
+            n2 = 1 if zp is not None else 2
+            for i in todo[:n2]:
+                done.append((i, second_product(i)))
+            todo = todo[n2:]
+            if zp is not None:
+                z_mult.append((s, (zp[0], zp[1], localise(zp[0], zp[1], cbanks))))
+        for i, acc in done:
+            store(i, acc)
+        for i in todo:
+            store(i, second_product(i))

@@ -18,10 +18,24 @@ FP4X4 = mybir.dt.float4_e2m1fn_x4
 MULT = mybir.AluOpType.mult
 COPY = mybir.ActivationFunctionType.Copy
 
-PREPS = [("y", 0), ("y", 1), ("x", 0), ("x", 1), ("x", 2), ("y", 2), ("y", 3), ("y", 4), ("y", 5), ("y", 6), ("y", 7), ("x", 3)]
+VECTOR_ONLY = {(1, 0), (8, 0), (6, 0), (4, 0)}
+PREPS = [("y", 0), ("x", 0), ("y", 1), ("y", 5), ("y", 2), ("y", 3), ("x", 2), ("y", 4), ("x", 1), ("y", 6), ("y", 7), ("x", 3)]
 SLOTS = [
-    (0, None), (1, None), (2, None), (3, (0, 0)), (4, (1, 0)), (5, (2, 0)), (6, None), (7, (0, 1)), (8, (1, 1)), (None, (2, 1)), (9, (0, 2)), (10, (1, 2)), (None, (2, 2)), (11, (0, 3)), (None, (1, 3)), (None, (2, 3)), (None, (3, 0)), (None, (3, 1)), (None, (3, 2)), (None, (3, 3)),
+    ((0, 1), ()),
+    ((2, 3), ()),
+    ((4, 5), ()),
+    ((6,), ((0, 0),)),
+    ((7, 8), ()),
+    ((), ((0, 1), (2, 2))),
+    ((9,), ((2, 1),)),
+    ((10,), ((1, 0), (0, 2))),
+    ((11,), ((1, 1), (2, 0))),
+    ((), ((2, 3), (1, 2))),
+    ((), ((3, 0), (3, 2))),
+    ((), ((0, 3), (1, 3))),
+    ((), ((3, 1), (3, 3))),
 ]
+N2 = 1
 
 
 def tile_localised_ensemble_covariance_d4_kernel(tc, x_bytes, x_scale, y_bytes, y_scale, rho, h_words, h_scales, out):
@@ -58,10 +72,10 @@ def tile_localised_ensemble_covariance_d4_kernel(tc, x_bytes, x_scale, y_bytes, 
             nc.sync.dma_start(out=t[:], in_=rho_rows[:, 2 * q : 2 * q + 2, 512 * g : 512 * g + 512])
             rho_t[q, g] = t
 
-        for pi, zp in SLOTS:
-            if pi is not None:
+        for pis, zps in SLOTS:
+            for pi in pis:
                 load(*PREPS[pi])
-            if zp is not None:
+            for zp in zps:
                 load_rho(*zp)
         hw = keep.tile([P, 4, 2 * R], U8, name="hw", align_bytes=64)
         nc.sync.dma_start(out=hw[:].bitcast(I32), in_=h_words.rearrange("g p c -> p g c").bitcast(I32))
@@ -91,7 +105,7 @@ def tile_localised_ensemble_covariance_d4_kernel(tc, x_bytes, x_scale, y_bytes, 
         widened = {}
 
         def on_vector(pi, a, g):
-            return g == 0 or (pi == 0 and a == 0) or (pi in (1, 2))
+            return g == 0 or (pi, a) in VECTOR_ONLY
 
         def widen(pi, engine):
             kind, j = PREPS[pi]
@@ -202,71 +216,91 @@ def tile_localised_ensemble_covariance_d4_kernel(tc, x_bytes, x_scale, y_bytes, 
                 in_=t[:].rearrange("p a r j -> p (a r j)"),
             )
 
+        def second_pass(i, g, acc, start, stop):
+            q, a = divmod(i, 2)
+            nc.tensor.matmul_mx(
+                out=acc[:],
+                lhsT=codes["z", q, g][:, 128 * a : 128 * a + 128].bitcast(FP8X4),
+                lhsT_scale=scales["z", q, g][:, 128 * a : 128 * a + 128],
+                rhs=hw[:, g, :].bitcast(FP4X4),
+                rhs_scale=hs[:, g, :],
+                start=start,
+                stop=stop,
+            )
+
         def second_product(i):
             acc = psum_a.tile([P, 512], F32, name="acc")
-            q, a = divmod(i, 2)
             for g in range(4):
-                nc.tensor.matmul_mx(
-                    out=acc[:],
-                    lhsT=codes["z", q, g][:, 128 * a : 128 * a + 128].bitcast(FP8X4),
-                    lhsT_scale=scales["z", q, g][:, 128 * a : 128 * a + 128],
-                    rhs=hw[:, g, :].bitcast(FP4X4),
-                    rhs_scale=hs[:, g, :],
-                    start=(g == 0),
-                    stop=(g == 3),
-                )
+                second_pass(i, g, acc, g == 0, g == 3)
             return acc
 
-        def store(i, acc):
+        def store(i, acc, on_vector=False):
             o = stage.tile([P, R], F32, name="o")
-            nc.scalar.copy(out=o[:], in_=acc[:])
+            if on_vector:
+                nc.vector.tensor_copy(out=o[:], in_=acc[:])
+            else:
+                nc.scalar.copy(out=o[:], in_=acc[:])
             nc.sync.dma_start(out=out[128 * i : 128 * i + 128, :], in_=o[:])
 
-        order = list(SLOTS) + [(None, None)] * (2 + 1)
-        widen(0, "v")
-        widen(0, "s")
-        turned = None
+        order = list(SLOTS) + [((), ())] * (2 + 1)
+        left = [4] * 4
+        for pis, zps in SLOTS:
+            for zp in zps:
+                last_pair = zp[0]
+        for pi in SLOTS[0][0]:
+            widen(pi, "v")
+            widen(pi, "s")
+        turned = []
         z_mult = []
-        z_turned = None
+        z_turned = []
         todo = []
         done = []
-        for s, (pi, zp) in enumerate(order):
-            nxt = order[s + 1][0] if s + 1 < len(order) else None
-            if nxt is not None:
-                widen(nxt, "v")
-                widen(nxt, "s")
-            if turned is not None:
-                quant_prep(turned)
-                turned = None
-            if z_turned is not None:
-                quant_z(*z_turned)
-                if z_turned[1] == 3:
-                    todo.extend([2 * z_turned[0], 2 * z_turned[0] + 1])
-                z_turned = None
-            z_now = None
-            if z_mult and (z_mult[0][0] <= s - 2 or (s >= len(SLOTS))):
-                z_now = z_mult.pop(0)[1]
-            if pi is not None:
-                banks = turn_prep(pi)
-            if z_now is not None:
-                zbank = turn_z(z_now[2])
-            if pi is not None:
-                empty_prep(pi, banks)
-                turned = pi
-            if z_now is not None:
-                z_turned = (z_now[0], z_now[1], empty_z(zbank))
+        open_acc = {}
+        open_g = []
+        passes = 0
+        for s, (pis, zps) in enumerate(order):
+            for pi in order[s + 1][0] if s + 1 < len(order) else ():
+                widen(pi, "v")
+                widen(pi, "s")
+            for pi in turned:
+                quant_prep(pi)
+            for q, g, zt in z_turned:
+                quant_z(q, g, zt)
+                left[q] -= 1
+                if q == last_pair:
+                    open_g.append(g)
+                elif left[q] == 0:
+                    todo.extend([2 * q, 2 * q + 1])
+            banks = [(pi, turn_prep(pi)) for pi in pis]
+            ready = [z for z in z_mult if z[0] <= s - 2 or s >= len(SLOTS)]
+            if s >= len(SLOTS):
+                ready = ready[:2]
+            z_mult = [z for z in z_mult if z not in ready]
+            zbanks = [(q, g, turn_z(zs)) for at, q, g, zs in ready]
+            for pi, b in banks:
+                empty_prep(pi, b)
+            turned = list(pis)
+            z_turned = [(q, g, empty_z(b)) for q, g, b in zbanks]
             for i, acc in done:
                 store(i, acc)
             done = []
-            if zp is not None:
-                cbanks = first_product(*zp)
-            n2 = 1 if zp is not None else 2
+            cbanks = [(q, g, first_product(q, g)) for q, g in zps]
+            n2 = N2 * max(1, len(zps)) if s < len(SLOTS) + 1 else 8
             for i in todo[:n2]:
                 done.append((i, second_product(i)))
             todo = todo[n2:]
-            if zp is not None:
-                z_mult.append((s, (zp[0], zp[1], localise(zp[0], zp[1], cbanks))))
-        for i, acc in done:
-            store(i, acc)
-        for i in todo:
-            store(i, second_product(i))
+            if s >= len(SLOTS) + 1 and open_g:
+                if not open_acc:
+                    for a in range(2):
+                        open_acc[a] = psum_a.tile([P, 512], F32, name="acc")
+                for a in range(2):
+                    for n, g in enumerate(open_g):
+                        second_pass(2 * last_pair + a, g, open_acc[a], passes + n == 0, passes + n == 3)
+                    if passes + len(open_g) == 4:
+                        done.append((2 * last_pair + a, open_acc[a]))
+                passes += len(open_g)
+                open_g = []
+            for q, g, b in cbanks:
+                z_mult.append((s, q, g, localise(q, g, b)))
+        for n, (i, acc) in enumerate(done):
+            store(i, acc, on_vector=(n == 0))

@@ -18,162 +18,178 @@ FP4X4 = mybir.dt.float4_e2m1fn_x4
 MULT = mybir.AluOpType.mult
 COPY = mybir.ActivationFunctionType.Copy
 
-VECTOR_ONLY = {(1, 0), (8, 0), (6, 0), (4, 0)}
-PREPS = [("y", 0), ("x", 0), ("y", 1), ("y", 5), ("y", 2), ("y", 3), ("x", 2), ("y", 4), ("x", 1), ("y", 6), ("y", 7), ("x", 3)]
-SLOTS = [
-    ((0, 1), ()),
-    ((2, 3), ()),
-    ((4, 5), ()),
-    ((6,), ((0, 0),)),
-    ((7, 8), ()),
-    ((), ((0, 1), (2, 2))),
-    ((9,), ((2, 1),)),
-    ((10,), ((1, 0), (0, 2))),
-    ((11,), ((1, 1), (2, 0))),
-    ((), ((2, 3), (1, 2))),
-    ((), ((3, 0), (3, 2))),
-    ((), ((0, 3), (1, 3))),
-    ((), ((3, 1), (3, 3))),
+STEPS = [
+    ((("y", 0), ("x", 3)), (), 0),
+    ((("y", 1), ("x", 1)), (), 0),
+    ((("x", 2), ("x", 0)), (), 1),
+    ((), ((3, 0), (1, 0)), 2),
+    ((("y", 3),), ((2, 0), (0, 0)), 1),
+    ((("y", 2), ("y", 4)), (), 1),
+    ((), ((1, 1), (0, 1)), 1),
+    ((("y", 5),), ((2, 1),), 2),
+    ((), ((3, 1), (1, 2)), 0),
+    ((("y", 6),), ((3, 2), (0, 2)), 2),
+    ((("y", 7),), (), 1),
+    ((), ((3, 3),), 2),
+    ((), ((1, 3), (2, 2)), 1),
+    ((), ((0, 3),), 0),
+    ((), ((2, 3),), 1),
 ]
-N2 = 1
+
+WIDENED_BY = {
+    ("x", 0): ("vv", "sv"),
+    ("x", 1): ("vs", "sv"),
+    ("x", 2): ("vv", "vv"),
+    ("x", 3): ("ss", "vv"),
+    ("y", 0): ("vs", "sv"),
+    ("y", 1): ("vv", "vv"),
+    ("y", 2): ("vs", "ss"),
+    ("y", 3): ("sv", "vv"),
+    ("y", 4): ("ss", "ss"),
+    ("y", 5): ("vs", "ss"),
+    ("y", 6): ("ss", "ss"),
+    ("y", 7): ("ss", "vs"),
+}
 
 
 def tile_localised_ensemble_covariance_d4_kernel(tc, x_bytes, x_scale, y_bytes, y_scale, rho, h_words, h_scales, out):
     nc = tc.nc
     with ExitStack() as ctx:
         keep = ctx.enter_context(tc.tile_pool(name="keep", bufs=1))
-        wide_pool = ctx.enter_context(tc.tile_pool(name="wide", bufs=6))
-        stage = ctx.enter_context(tc.tile_pool(name="stage", bufs=3))
-        psum_t = ctx.enter_context(tc.psum_pool(name="psum_t", bufs=4))
-        psum_a = ctx.enter_context(tc.psum_pool(name="psum_a", bufs=4))
+        wide_pool = ctx.enter_context(tc.tile_pool(name="wide", bufs=8))
+        stage = ctx.enter_context(tc.tile_pool(name="stage", bufs=4))
+        psum_turn = ctx.enter_context(tc.psum_pool(name="psum_turn", bufs=4))
+        psum_acc = ctx.enter_context(tc.psum_pool(name="psum_acc", bufs=4))
         ctx.enter_context(tc.manual_schedule())
 
-        ysc = keep.tile([P, 16, 8], F32, name="ysc")
-        nc.scalar.dma_start(out=ysc[:].rearrange("p b k -> p (b k)"), in_=y_scale.rearrange("b k -> (b k)").partition_broadcast(P))
-        xsc = keep.tile([P, 8, 8], F32, name="xsc")
-        nc.scalar.dma_start(out=xsc[:], in_=x_scale.rearrange("(i p) k -> p i k", p=P))
+        y_scales = keep.tile([P, 16, 8], F32, name="y_scales")
+        nc.scalar.dma_start(out=y_scales[:].rearrange("p b k -> p (b k)"), in_=y_scale.rearrange("b k -> (b k)").partition_broadcast(P))
+        x_scales = keep.tile([P, 8, 8], F32, name="x_scales")
+        nc.scalar.dma_start(out=x_scales[:], in_=x_scale.rearrange("(i p) k -> p i k", p=P))
 
-        src = {"x": x_bytes.rearrange("(u p) k -> p u k", p=P), "y": y_bytes.rearrange("(u p) k -> p u k", p=P)}
-        raw = {}
+        byte_rows = {"x": x_bytes.rearrange("(i p) k -> p i k", p=P), "y": y_bytes.rearrange("(i p) k -> p i k", p=P)}
         rho_rows = rho.rearrange("(i p) n -> p i n", p=P)
-        rho_t = {}
-
-        def load(kind, j):
-            t = keep.tile([P, 2, M], U8, name=f"raw_{kind}{j}")
-            if (kind, j) == ("y", 0):
-                for a in range(2):
-                    nc.sync.dma_start(out=t[:, a, :], in_=src[kind][:, 2 * j + a, :])
-            else:
-                nc.sync.dma_start(out=t[:], in_=src[kind][:, 2 * j : 2 * j + 2, :])
-            raw[kind, j] = t
-
-        def load_rho(q, g):
-            t = keep.tile([P, 2, 512], BF16, name=f"rho_{q}_{g}")
-            nc.sync.dma_start(out=t[:], in_=rho_rows[:, 2 * q : 2 * q + 2, 512 * g : 512 * g + 512])
-            rho_t[q, g] = t
-
-        for pis, zps in SLOTS:
-            for pi in pis:
-                load(*PREPS[pi])
-            for zp in zps:
-                load_rho(*zp)
-        hw = keep.tile([P, 4, 2 * R], U8, name="hw", align_bytes=64)
-        nc.sync.dma_start(out=hw[:].bitcast(I32), in_=h_words.rearrange("g p c -> p g c").bitcast(I32))
-        hs = keep.tile([P, 4, R], U8, name="hs", align_bytes=64)
-        nc.gpsimd.memset(hs[:].bitcast(I32), 0)
+        raw = {}
+        weights = {}
+        first_pair = STEPS[0][0][0]
+        for pairs, panels, n_out in STEPS:
+            for kind, j in pairs:
+                raw_pair = keep.tile([P, 2, M], U8, name=f"raw_{kind}{j}")
+                if (kind, j) == first_pair:
+                    for a in range(2):
+                        nc.sync.dma_start(out=raw_pair[:, a, :], in_=byte_rows[kind][:, 2 * j + a, :])
+                else:
+                    nc.sync.dma_start(out=raw_pair[:], in_=byte_rows[kind][:, 2 * j : 2 * j + 2, :])
+                raw[kind, j] = raw_pair
+            for q, g in panels:
+                weights_panel = keep.tile([P, 2, 512], BF16, name=f"rho_{q}{g}")
+                nc.sync.dma_start(out=weights_panel[:], in_=rho_rows[:, 2 * q : 2 * q + 2, 512 * g : 512 * g + 512])
+                weights[q, g] = weights_panel
+        h_codes = keep.tile([P, 4, 2 * R], U8, name="h_codes", align_bytes=64)
+        nc.sync.dma_start(out=h_codes[:].bitcast(I32), in_=h_words.rearrange("g p c -> p g c").bitcast(I32))
+        h_plane = keep.tile([P, 4, R], U8, name="h_plane", align_bytes=64)
+        nc.gpsimd.memset(h_plane[:].bitcast(I32), 0)
         for quad in range(4):
             nc.sync.dma_start(
-                out=hs[32 * quad : 32 * quad + 4, :, :].bitcast(I32),
-                in_=h_scales[:, 4 * quad : 4 * quad + 4, :].rearrange("g q n -> q g n").bitcast(I32),
+                out=h_plane[32 * quad : 32 * quad + 4, :, :].bitcast(I32),
+                in_=h_scales[:, 4 * quad : 4 * quad + 4, :].rearrange("g r n -> r g n").bitcast(I32),
             )
 
-        ident = keep.tile([P, P], F32, name="ident")
-        make_identity(nc, ident[:])
+        identity = keep.tile([P, P], F32, name="identity")
+        make_identity(nc, identity[:])
 
         codes = {}
-        scales = {}
+        planes = {}
+
+        def operand(key, shape, name):
+            codes[key] = keep.tile(shape, U32, name=f"codes_{name}", align_bytes=64)
+            planes[key] = keep.tile(shape, U8, name=f"plane_{name}", align_bytes=64)
+
         for g in range(4):
-            codes["y", g] = keep.tile([P, 2, 512], U32, name=f"yq{g}", align_bytes=64)
-            scales["y", g] = keep.tile([P, 2, 512], U8, name=f"ys{g}", align_bytes=64)
+            operand(("y", g), [P, 2, 512], f"y{g}")
         for q in range(4):
-            codes["x", q] = keep.tile([P, 2, 256], U32, name=f"xq{q}", align_bytes=64)
-            scales["x", q] = keep.tile([P, 2, 256], U8, name=f"xs{q}", align_bytes=64)
+            operand(("x", q), [P, 2, 256], f"x{q}")
             for g in range(4):
-                codes["z", q, g] = keep.tile([P, 256], U32, name=f"zq{q}{g}", align_bytes=64)
-                scales["z", q, g] = keep.tile([P, 256], U8, name=f"zs{q}{g}", align_bytes=64)
+                operand(("z", q, g), [P, 256], f"z{q}{g}")
 
         widened = {}
-
-        def on_vector(pi, a, g):
-            return g == 0 or (pi, a) in VECTOR_ONLY
-
-        def widen(pi, engine):
-            kind, j = PREPS[pi]
-            for a in range(2):
-                if (pi, a) not in widened:
-                    widened[pi, a] = wide_pool.tile([P, 2, 512], BF16, name="wide", align_bytes=64)
-                w = widened[pi, a]
-                for g in range(2):
-                    if on_vector(pi, a, g) != (engine == "v"):
-                        continue
-                    for b in range(4):
-                        k0 = 512 * g + 128 * b
-                        src_ap = raw[kind, j][:, a, k0 : k0 + 128].bitcast(FP8)
-                        sc = ysc if kind == "y" else xsc
-                        s_ap = sc[:, 2 * j + a, 4 * g + b : 4 * g + b + 1]
-                        if engine == "v":
-                            dst = w[:, g, :].rearrange("p (u q e) -> p q u e", u=2, e=2)[:, 32 * b : 32 * b + 32, :, :]
-                            nc.vector.tensor_scalar(out=dst, in0=src_ap.rearrange("p (q u e) -> p q u e", u=2, e=2), scalar1=s_ap, scalar2=None, op0=MULT)
-                        else:
-                            nc.scalar.activation(out=w[:, g, 128 * b : 128 * b + 128], in_=src_ap, func=COPY, scale=s_ap)
-
         grouped = {}
 
-        def turn_prep(pi):
+        def widen(pair):
+            kind, j = pair
+            scale_tile = x_scales if kind == "x" else y_scales
+            widened[pair] = [wide_pool.tile([P, 2, 512], BF16, name="wide", align_bytes=64) for a in range(2)]
+            for engine in "vs":
+                for a in range(2):
+                    wide = widened[pair][a]
+                    for g in range(2):
+                        if WIDENED_BY[pair][a][g] != engine:
+                            continue
+                        for b in range(4):
+                            m0 = 512 * g + 128 * b
+                            values = raw[pair][:, a, m0 : m0 + 128].bitcast(FP8)
+                            scale = scale_tile[:, 2 * j + a, m0 // 128 : m0 // 128 + 1]
+                            if engine == "v":
+                                by_word = wide[:, g, :].rearrange("r (u p e) -> r p u e", u=2, e=2)
+                                nc.vector.tensor_scalar(
+                                    out=by_word[:, 32 * b : 32 * b + 32, :, :],
+                                    in0=values.rearrange("r (p u e) -> r p u e", u=2, e=2),
+                                    scalar1=scale,
+                                    scalar2=None,
+                                    op0=MULT,
+                                )
+                            else:
+                                nc.scalar.activation(out=wide[:, g, 128 * b : 128 * b + 128], in_=values, func=COPY, scale=scale)
+
+        def turn_pair(pair):
             banks = []
             for a in range(2):
-                bank = psum_t.tile([P, 2, 2, P], F32, name="turn")
-                words = widened[pi, a][:].bitcast(F32)
+                bank = psum_turn.tile([P, 2, 2, P], F32, name="turn")
+                words = widened[pair][a][:].bitcast(F32)
                 for g in range(2):
                     for u in range(2):
-                        if on_vector(pi, a, g):
-                            s = words[:, g, 128 * u : 128 * u + 128]
+                        if WIDENED_BY[pair][a][g] == "v":
+                            part = words[:, g, 128 * u : 128 * u + 128]
                         else:
-                            s = words[:, g, u : 256 : 2]
-                        nc.tensor.transpose(bank[:, g, u, :], s, ident[:])
+                            part = words[:, g, u : 256 : 2]
+                        nc.tensor.transpose(bank[:, g, u, :], part, identity[:])
                 banks.append(bank)
             return banks
 
-        def empty_prep(pi, banks):
-            t = stage.tile([P, 2, 2, P, 4], BF16, name="grouped", align_bytes=64)
+        def empty_pair(pair, banks):
+            grouped[pair] = stage.tile([P, 2, 2, P, 4], BF16, name="grouped", align_bytes=64)
             for a in range(2):
-                nc.scalar.copy(
-                    out=t[:, :, a, :, :].bitcast(F32),
-                    in_=banks[a][:].rearrange("p g u r -> p g r u"),
-                )
-            grouped[pi] = t
+                nc.scalar.copy(out=grouped[pair][:, :, a, :, :].bitcast(F32), in_=banks[a][:].rearrange("p g u r -> p g r u"))
 
-        def quant_prep(pi):
-            kind, j = PREPS[pi]
-            key, c0 = (("y", j // 2), 256 * (j % 2)) if kind == "y" else (("x", j), 0)
+        def quantise_pair(pair):
+            kind, j = pair
+            if kind == "x":
+                nc.vector.quantize_mx(
+                    out=codes["x", j][:].rearrange("p g r -> p (g r)").bitcast(FP8X4),
+                    scales=planes["x", j][:].rearrange("p g r -> p (g r)"),
+                    in_=grouped[pair][:].rearrange("p g a r t -> p (g a r t)"),
+                )
+                return
+            rows = slice(256 * (j % 2), 256 * (j % 2) + 256)
             for g in range(2):
                 nc.vector.quantize_mx(
-                    out=codes[key][:, g, c0 : c0 + 256].bitcast(FP8X4),
-                    scales=scales[key][:, g, c0 : c0 + 256],
-                    in_=grouped[pi][:, g, :, :, :].rearrange("p a r j -> p (a r j)"),
+                    out=codes["y", j // 2][:, g, rows].bitcast(FP8X4),
+                    scales=planes["y", j // 2][:, g, rows],
+                    in_=grouped[pair][:, g, :, :, :].rearrange("p a r t -> p (a r t)"),
                 )
 
         def first_product(q, g):
             banks = []
             for a in range(2):
-                acc = psum_a.tile([P, 512], F32, name="acc")
+                acc = psum_acc.tile([P, 512], F32, name="acc")
+                rows = slice(128 * a, 128 * a + 128)
                 for k in range(2):
                     nc.tensor.matmul_mx(
                         out=acc[:],
-                        lhsT=codes["x", q][:, k, 128 * a : 128 * a + 128].bitcast(FP8X4),
-                        lhsT_scale=scales["x", q][:, k, 128 * a : 128 * a + 128],
+                        lhsT=codes["x", q][:, k, rows].bitcast(FP8X4),
+                        lhsT_scale=planes["x", q][:, k, rows],
                         rhs=codes["y", g][:, k, :].bitcast(FP8X4),
-                        rhs_scale=scales["y", g][:, k, :],
+                        rhs_scale=planes["y", g][:, k, :],
                         start=(k == 0),
                         stop=(k == 1),
                     )
@@ -181,126 +197,124 @@ def tile_localised_ensemble_covariance_d4_kernel(tc, x_bytes, x_scale, y_bytes, 
             return banks
 
         def localise(q, g, banks):
-            zs = []
+            tiles = []
             for a in range(2):
                 z = stage.tile([P, 2, 256], BF16, name=f"z{a}", align_bytes=64)
                 for u in range(2):
                     nc.vector.scalar_tensor_tensor(
-                        out=z[:, u, :].rearrange("p (q e) -> p q e", e=2),
-                        in0=banks[a][:].rearrange("p (q u e) -> p u q e", u=2, e=2)[:, u, :, :],
+                        out=z[:, u, :].rearrange("r (p e) -> r p e", e=2),
+                        in0=banks[a][:].rearrange("r (p u e) -> r u p e", u=2, e=2)[:, u, :, :],
                         scalar=1.0 / (M - 1),
-                        in1=rho_t[q, g][:, a, :].rearrange("p (q u e) -> p u q e", u=2, e=2)[:, u, :, :],
+                        in1=weights[q, g][:, a, :].rearrange("r (p u e) -> r u p e", u=2, e=2)[:, u, :, :],
                         op0=MULT,
                         op1=MULT,
                     )
-                zs.append(z)
-            return zs
+                tiles.append(z)
+            return tiles
 
-        def turn_z(zs):
-            bank = psum_t.tile([P, 2, 2, P], F32, name="turn")
+        def turn_panel(tiles):
+            bank = psum_turn.tile([P, 2, 2, P], F32, name="turn")
             for a in range(2):
-                words = zs[a][:].bitcast(F32)
+                words = tiles[a][:].bitcast(F32)
                 for u in range(2):
-                    nc.tensor.transpose(bank[:, a, u, :], words[:, u, :], ident[:])
+                    nc.tensor.transpose(bank[:, a, u, :], words[:, u, :], identity[:])
             return bank
 
-        def empty_z(bank):
-            t = stage.tile([P, 2, P, 4], BF16, name="zgrouped", align_bytes=64)
-            nc.scalar.copy(out=t[:].bitcast(F32), in_=bank[:].rearrange("p a u r -> p a r u"))
-            return t
+        def empty_panel(bank):
+            z_grouped = stage.tile([P, 2, P, 4], BF16, name="z_grouped", align_bytes=64)
+            nc.scalar.copy(out=z_grouped[:].bitcast(F32), in_=bank[:].rearrange("p a u r -> p a r u"))
+            return z_grouped
 
-        def quant_z(q, g, t):
+        def quantise_panel(q, g, z_grouped):
             nc.vector.quantize_mx(
                 out=codes["z", q, g][:].bitcast(FP8X4),
-                scales=scales["z", q, g][:],
-                in_=t[:].rearrange("p a r j -> p (a r j)"),
+                scales=planes["z", q, g][:],
+                in_=z_grouped[:].rearrange("p a r t -> p (a r t)"),
             )
 
         def second_pass(i, g, acc, start, stop):
             q, a = divmod(i, 2)
+            rows = slice(128 * a, 128 * a + 128)
             nc.tensor.matmul_mx(
                 out=acc[:],
-                lhsT=codes["z", q, g][:, 128 * a : 128 * a + 128].bitcast(FP8X4),
-                lhsT_scale=scales["z", q, g][:, 128 * a : 128 * a + 128],
-                rhs=hw[:, g, :].bitcast(FP4X4),
-                rhs_scale=hs[:, g, :],
+                lhsT=codes["z", q, g][:, rows].bitcast(FP8X4),
+                lhsT_scale=planes["z", q, g][:, rows],
+                rhs=h_codes[:, g, :].bitcast(FP4X4),
+                rhs_scale=h_plane[:, g, :],
                 start=start,
                 stop=stop,
             )
 
         def second_product(i):
-            acc = psum_a.tile([P, 512], F32, name="acc")
+            acc = psum_acc.tile([P, R], F32, name="acc")
             for g in range(4):
                 second_pass(i, g, acc, g == 0, g == 3)
             return acc
 
         def store(i, acc, on_vector=False):
-            o = stage.tile([P, R], F32, name="o")
+            rows = stage.tile([P, R], F32, name="out_rows")
             if on_vector:
-                nc.vector.tensor_copy(out=o[:], in_=acc[:])
+                nc.vector.tensor_copy(out=rows[:], in_=acc[:])
             else:
-                nc.scalar.copy(out=o[:], in_=acc[:])
-            nc.sync.dma_start(out=out[128 * i : 128 * i + 128, :], in_=o[:])
+                nc.scalar.copy(out=rows[:], in_=acc[:])
+            nc.sync.dma_start(out=out[128 * i : 128 * i + 128, :], in_=rows[:])
 
-        order = list(SLOTS) + [((), ())] * (2 + 1)
-        left = [4] * 4
-        for pis, zps in SLOTS:
-            for zp in zps:
-                last_pair = zp[0]
-        for pi in SLOTS[0][0]:
-            widen(pi, "v")
-            widen(pi, "s")
-        turned = []
-        z_mult = []
-        z_turned = []
-        todo = []
-        done = []
-        open_acc = {}
-        open_g = []
-        passes = 0
-        for s, (pis, zps) in enumerate(order):
-            for pi in order[s + 1][0] if s + 1 < len(order) else ():
-                widen(pi, "v")
-                widen(pi, "s")
-            for pi in turned:
-                quant_prep(pi)
-            for q, g, zt in z_turned:
-                quant_z(q, g, zt)
-                left[q] -= 1
-                if q == last_pair:
-                    open_g.append(g)
-                elif left[q] == 0:
-                    todo.extend([2 * q, 2 * q + 1])
-            banks = [(pi, turn_prep(pi)) for pi in pis]
-            ready = [z for z in z_mult if z[0] <= s - 2 or s >= len(SLOTS)]
-            if s >= len(SLOTS):
-                ready = ready[:2]
-            z_mult = [z for z in z_mult if z not in ready]
-            zbanks = [(q, g, turn_z(zs)) for at, q, g, zs in ready]
-            for pi, b in banks:
-                empty_prep(pi, b)
-            turned = list(pis)
-            z_turned = [(q, g, empty_z(b)) for q, g, b in zbanks]
-            for i, acc in done:
+        last_q = STEPS[-1][1][-1][0]
+        n_steps = len(STEPS)
+        steps = STEPS + [((), (), 2), ((), (), 8), ((), (), 8)]
+        turned_pairs = []
+        turned_panels = []
+        localised = []
+        panels_missing = [4, 4, 4, 4]
+        ready = []
+        summed = []
+        last_acc = []
+        last_panels = []
+        n_summed = 0
+        for pair in STEPS[0][0]:
+            widen(pair)
+        for s, (pairs, panels, n_out) in enumerate(steps):
+            for pair in steps[s + 1][0] if s + 1 < len(steps) else ():
+                widen(pair)
+            for pair in turned_pairs:
+                quantise_pair(pair)
+            for q, g, z_grouped in turned_panels:
+                quantise_panel(q, g, z_grouped)
+                panels_missing[q] -= 1
+                if q == last_q:
+                    last_panels.append(g)
+                elif panels_missing[q] == 0:
+                    ready.extend([2 * q, 2 * q + 1])
+
+            pair_banks = [turn_pair(pair) for pair in pairs]
+            due = [entry for entry in localised if entry[0] <= s - 2 or s >= n_steps]
+            if s >= n_steps:
+                due = due[:2]
+            localised = [entry for entry in localised if entry not in due]
+            panel_banks = [turn_panel(tiles) for made, q, g, tiles in due]
+            for pair, banks in zip(pairs, pair_banks):
+                empty_pair(pair, banks)
+            turned_pairs = pairs
+            turned_panels = [(q, g, empty_panel(bank)) for (made, q, g, tiles), bank in zip(due, panel_banks)]
+            for i, acc in summed:
                 store(i, acc)
-            done = []
-            cbanks = [(q, g, first_product(q, g)) for q, g in zps]
-            n2 = N2 * max(1, len(zps)) if s < len(SLOTS) + 1 else 8
-            for i in todo[:n2]:
-                done.append((i, second_product(i)))
-            todo = todo[n2:]
-            if s >= len(SLOTS) + 1 and open_g:
-                if not open_acc:
+
+            products = [first_product(q, g) for q, g in panels]
+            summed = [(i, second_product(i)) for i in ready[:n_out]]
+            ready = ready[n_out:]
+            if s > n_steps and last_panels:
+                if not last_acc:
                     for a in range(2):
-                        open_acc[a] = psum_a.tile([P, 512], F32, name="acc")
+                        acc = psum_acc.tile([P, R], F32, name="acc")
+                        last_acc.append(acc)
                 for a in range(2):
-                    for n, g in enumerate(open_g):
-                        second_pass(2 * last_pair + a, g, open_acc[a], passes + n == 0, passes + n == 3)
-                    if passes + len(open_g) == 4:
-                        done.append((2 * last_pair + a, open_acc[a]))
-                passes += len(open_g)
-                open_g = []
-            for q, g, b in cbanks:
-                z_mult.append((s, q, g, localise(q, g, b)))
-        for n, (i, acc) in enumerate(done):
+                    for n, g in enumerate(last_panels, n_summed):
+                        second_pass(2 * last_q + a, g, last_acc[a], n == 0, n == 3)
+                n_summed += len(last_panels)
+                last_panels = []
+                if n_summed == 4:
+                    summed.extend((2 * last_q + a, last_acc[a]) for a in range(2))
+            for (q, g), banks in zip(panels, products):
+                localised.append((s, q, g, localise(q, g, banks)))
+        for n, (i, acc) in enumerate(summed):
             store(i, acc, on_vector=(n == 0))

from contextlib import ExitStack

import concourse.mybir as mybir
from concourse.masks import make_identity

T, N, M, R = 1024, 2048, 1024, 512
P = 128
FLOPS = 2 * T * N * M + 2 * T * N * R

F32 = mybir.dt.float32
BF16 = mybir.dt.bfloat16
I32 = mybir.dt.int32
U32 = mybir.dt.uint32
U8 = mybir.dt.uint8
FP8 = mybir.dt.float8_e4m3fn
FP8X4 = mybir.dt.float8_e4m3fn_x4
FP4X4 = mybir.dt.float4_e2m1fn_x4
MULT = mybir.AluOpType.mult
COPY = mybir.ActivationFunctionType.Copy

STEPS = [
    ((("y", 0), ("x", 3)), (), 0),
    ((("y", 1), ("x", 1)), (), 0),
    ((("x", 2), ("x", 0)), (), 1),
    ((), ((3, 0), (1, 0)), 2),
    ((("y", 3),), ((2, 0), (0, 0)), 1),
    ((("y", 2), ("y", 4)), (), 1),
    ((), ((1, 1), (0, 1)), 1),
    ((("y", 5),), ((2, 1),), 2),
    ((), ((3, 1), (1, 2)), 0),
    ((("y", 6),), ((3, 2), (0, 2)), 2),
    ((("y", 7),), (), 1),
    ((), ((3, 3),), 2),
    ((), ((1, 3), (2, 2)), 1),
    ((), ((0, 3),), 0),
    ((), ((2, 3),), 1),
]

WIDENED_BY = {
    ("x", 0): ("vv", "sv"),
    ("x", 1): ("vs", "sv"),
    ("x", 2): ("vv", "vv"),
    ("x", 3): ("ss", "vv"),
    ("y", 0): ("vs", "sv"),
    ("y", 1): ("vv", "vv"),
    ("y", 2): ("vs", "ss"),
    ("y", 3): ("sv", "vv"),
    ("y", 4): ("ss", "ss"),
    ("y", 5): ("vs", "ss"),
    ("y", 6): ("ss", "ss"),
    ("y", 7): ("ss", "vs"),
}


def tile_localised_ensemble_covariance_d4_kernel(tc, x_bytes, x_scale, y_bytes, y_scale, rho, h_words, h_scales, out):
    nc = tc.nc
    with ExitStack() as ctx:
        keep = ctx.enter_context(tc.tile_pool(name="keep", bufs=1))
        wide_pool = ctx.enter_context(tc.tile_pool(name="wide", bufs=8))
        stage = ctx.enter_context(tc.tile_pool(name="stage", bufs=4))
        psum_turn = ctx.enter_context(tc.psum_pool(name="psum_turn", bufs=4))
        psum_acc = ctx.enter_context(tc.psum_pool(name="psum_acc", bufs=4))
        ctx.enter_context(tc.manual_schedule())

        y_scales = keep.tile([P, 16, 8], F32, name="y_scales")
        nc.scalar.dma_start(out=y_scales[:].rearrange("p b k -> p (b k)"), in_=y_scale.rearrange("b k -> (b k)").partition_broadcast(P))
        x_scales = keep.tile([P, 8, 8], F32, name="x_scales")
        nc.scalar.dma_start(out=x_scales[:], in_=x_scale.rearrange("(i p) k -> p i k", p=P))

        byte_rows = {"x": x_bytes.rearrange("(i p) k -> p i k", p=P), "y": y_bytes.rearrange("(i p) k -> p i k", p=P)}
        rho_rows = rho.rearrange("(i p) n -> p i n", p=P)
        raw = {}
        weights = {}
        first_pair = STEPS[0][0][0]
        for pairs, panels, n_out in STEPS:
            for kind, j in pairs:
                raw_pair = keep.tile([P, 2, M], U8, name=f"raw_{kind}{j}")
                if (kind, j) == first_pair:
                    for a in range(2):
                        nc.sync.dma_start(out=raw_pair[:, a, :], in_=byte_rows[kind][:, 2 * j + a, :])
                else:
                    nc.sync.dma_start(out=raw_pair[:], in_=byte_rows[kind][:, 2 * j : 2 * j + 2, :])
                raw[kind, j] = raw_pair
            for q, g in panels:
                weights_panel = keep.tile([P, 2, 512], BF16, name=f"rho_{q}{g}")
                nc.sync.dma_start(out=weights_panel[:], in_=rho_rows[:, 2 * q : 2 * q + 2, 512 * g : 512 * g + 512])
                weights[q, g] = weights_panel
        h_codes = keep.tile([P, 4, 2 * R], U8, name="h_codes", align_bytes=64)
        nc.sync.dma_start(out=h_codes[:].bitcast(I32), in_=h_words.rearrange("g p c -> p g c").bitcast(I32))
        h_plane = keep.tile([P, 4, R], U8, name="h_plane", align_bytes=64)
        nc.gpsimd.memset(h_plane[:].bitcast(I32), 0)
        for quad in range(4):
            nc.sync.dma_start(
                out=h_plane[32 * quad : 32 * quad + 4, :, :].bitcast(I32),
                in_=h_scales[:, 4 * quad : 4 * quad + 4, :].rearrange("g r n -> r g n").bitcast(I32),
            )

        identity = keep.tile([P, P], F32, name="identity")
        make_identity(nc, identity[:])

        codes = {}
        planes = {}

        def operand(key, shape, name):
            codes[key] = keep.tile(shape, U32, name=f"codes_{name}", align_bytes=64)
            planes[key] = keep.tile(shape, U8, name=f"plane_{name}", align_bytes=64)

        for g in range(4):
            operand(("y", g), [P, 2, 512], f"y{g}")
        for q in range(4):
            operand(("x", q), [P, 2, 256], f"x{q}")
            for g in range(4):
                operand(("z", q, g), [P, 256], f"z{q}{g}")

        widened = {}
        grouped = {}

        def widen(pair):
            kind, j = pair
            scale_tile = x_scales if kind == "x" else y_scales
            widened[pair] = [wide_pool.tile([P, 2, 512], BF16, name="wide", align_bytes=64) for a in range(2)]
            for engine in "vs":
                for a in range(2):
                    wide = widened[pair][a]
                    for g in range(2):
                        if WIDENED_BY[pair][a][g] != engine:
                            continue
                        for b in range(4):
                            m0 = 512 * g + 128 * b
                            values = raw[pair][:, a, m0 : m0 + 128].bitcast(FP8)
                            scale = scale_tile[:, 2 * j + a, m0 // 128 : m0 // 128 + 1]
                            if engine == "v":
                                by_word = wide[:, g, :].rearrange("r (u p e) -> r p u e", u=2, e=2)
                                nc.vector.tensor_scalar(
                                    out=by_word[:, 32 * b : 32 * b + 32, :, :],
                                    in0=values.rearrange("r (p u e) -> r p u e", u=2, e=2),
                                    scalar1=scale,
                                    scalar2=None,
                                    op0=MULT,
                                )
                            else:
                                nc.scalar.activation(out=wide[:, g, 128 * b : 128 * b + 128], in_=values, func=COPY, scale=scale)

        def turn_pair(pair):
            banks = []
            for a in range(2):
                bank = psum_turn.tile([P, 2, 2, P], F32, name="turn")
                words = widened[pair][a][:].bitcast(F32)
                for g in range(2):
                    for u in range(2):
                        if WIDENED_BY[pair][a][g] == "v":
                            part = words[:, g, 128 * u : 128 * u + 128]
                        else:
                            part = words[:, g, u : 256 : 2]
                        nc.tensor.transpose(bank[:, g, u, :], part, identity[:])
                banks.append(bank)
            return banks

        def empty_pair(pair, banks):
            grouped[pair] = stage.tile([P, 2, 2, P, 4], BF16, name="grouped", align_bytes=64)
            for a in range(2):
                nc.scalar.copy(out=grouped[pair][:, :, a, :, :].bitcast(F32), in_=banks[a][:].rearrange("p g u r -> p g r u"))

        def quantise_pair(pair):
            kind, j = pair
            if kind == "x":
                nc.vector.quantize_mx(
                    out=codes["x", j][:].rearrange("p g r -> p (g r)").bitcast(FP8X4),
                    scales=planes["x", j][:].rearrange("p g r -> p (g r)"),
                    in_=grouped[pair][:].rearrange("p g a r t -> p (g a r t)"),
                )
                return
            rows = slice(256 * (j % 2), 256 * (j % 2) + 256)
            for g in range(2):
                nc.vector.quantize_mx(
                    out=codes["y", j // 2][:, g, rows].bitcast(FP8X4),
                    scales=planes["y", j // 2][:, g, rows],
                    in_=grouped[pair][:, g, :, :, :].rearrange("p a r t -> p (a r t)"),
                )

        def first_product(q, g):
            banks = []
            for a in range(2):
                acc = psum_acc.tile([P, 512], F32, name="acc")
                rows = slice(128 * a, 128 * a + 128)
                for k in range(2):
                    nc.tensor.matmul_mx(
                        out=acc[:],
                        lhsT=codes["x", q][:, k, rows].bitcast(FP8X4),
                        lhsT_scale=planes["x", q][:, k, rows],
                        rhs=codes["y", g][:, k, :].bitcast(FP8X4),
                        rhs_scale=planes["y", g][:, k, :],
                        start=(k == 0),
                        stop=(k == 1),
                    )
                banks.append(acc)
            return banks

        def localise(q, g, banks):
            tiles = []
            for a in range(2):
                z = stage.tile([P, 2, 256], BF16, name=f"z{a}", align_bytes=64)
                for u in range(2):
                    nc.vector.scalar_tensor_tensor(
                        out=z[:, u, :].rearrange("r (p e) -> r p e", e=2),
                        in0=banks[a][:].rearrange("r (p u e) -> r u p e", u=2, e=2)[:, u, :, :],
                        scalar=1.0 / (M - 1),
                        in1=weights[q, g][:, a, :].rearrange("r (p u e) -> r u p e", u=2, e=2)[:, u, :, :],
                        op0=MULT,
                        op1=MULT,
                    )
                tiles.append(z)
            return tiles

        def turn_panel(tiles):
            bank = psum_turn.tile([P, 2, 2, P], F32, name="turn")
            for a in range(2):
                words = tiles[a][:].bitcast(F32)
                for u in range(2):
                    nc.tensor.transpose(bank[:, a, u, :], words[:, u, :], identity[:])
            return bank

        def empty_panel(bank):
            z_grouped = stage.tile([P, 2, P, 4], BF16, name="z_grouped", align_bytes=64)
            nc.scalar.copy(out=z_grouped[:].bitcast(F32), in_=bank[:].rearrange("p a u r -> p a r u"))
            return z_grouped

        def quantise_panel(q, g, z_grouped):
            nc.vector.quantize_mx(
                out=codes["z", q, g][:].bitcast(FP8X4),
                scales=planes["z", q, g][:],
                in_=z_grouped[:].rearrange("p a r t -> p (a r t)"),
            )

        def second_pass(i, g, acc, start, stop):
            q, a = divmod(i, 2)
            rows = slice(128 * a, 128 * a + 128)
            nc.tensor.matmul_mx(
                out=acc[:],
                lhsT=codes["z", q, g][:, rows].bitcast(FP8X4),
                lhsT_scale=planes["z", q, g][:, rows],
                rhs=h_codes[:, g, :].bitcast(FP4X4),
                rhs_scale=h_plane[:, g, :],
                start=start,
                stop=stop,
            )

        def second_product(i):
            acc = psum_acc.tile([P, R], F32, name="acc")
            for g in range(4):
                second_pass(i, g, acc, g == 0, g == 3)
            return acc

        def store(i, acc, on_vector=False):
            rows = stage.tile([P, R], F32, name="out_rows")
            if on_vector:
                nc.vector.tensor_copy(out=rows[:], in_=acc[:])
            else:
                nc.scalar.copy(out=rows[:], in_=acc[:])
            nc.sync.dma_start(out=out[128 * i : 128 * i + 128, :], in_=rows[:])

        last_q = STEPS[-1][1][-1][0]
        n_steps = len(STEPS)
        steps = STEPS + [((), (), 2), ((), (), 8), ((), (), 8)]
        turned_pairs = []
        turned_panels = []
        localised = []
        panels_missing = [4, 4, 4, 4]
        ready = []
        summed = []
        last_acc = []
        last_panels = []
        n_summed = 0
        for pair in STEPS[0][0]:
            widen(pair)
        for s, (pairs, panels, n_out) in enumerate(steps):
            for pair in steps[s + 1][0] if s + 1 < len(steps) else ():
                widen(pair)
            for pair in turned_pairs:
                quantise_pair(pair)
            for q, g, z_grouped in turned_panels:
                quantise_panel(q, g, z_grouped)
                panels_missing[q] -= 1
                if q == last_q:
                    last_panels.append(g)
                elif panels_missing[q] == 0:
                    ready.extend([2 * q, 2 * q + 1])

            pair_banks = [turn_pair(pair) for pair in pairs]
            due = [entry for entry in localised if entry[0] <= s - 2 or s >= n_steps]
            if s >= n_steps:
                due = due[:2]
            localised = [entry for entry in localised if entry not in due]
            panel_banks = [turn_panel(tiles) for made, q, g, tiles in due]
            for pair, banks in zip(pairs, pair_banks):
                empty_pair(pair, banks)
            turned_pairs = pairs
            turned_panels = [(q, g, empty_panel(bank)) for (made, q, g, tiles), bank in zip(due, panel_banks)]
            for i, acc in summed:
                store(i, acc)

            products = [first_product(q, g) for q, g in panels]
            summed = [(i, second_product(i)) for i in ready[:n_out]]
            ready = ready[n_out:]
            if s > n_steps and last_panels:
                if not last_acc:
                    for a in range(2):
                        acc = psum_acc.tile([P, R], F32, name="acc")
                        last_acc.append(acc)
                for a in range(2):
                    for n, g in enumerate(last_panels, n_summed):
                        second_pass(2 * last_q + a, g, last_acc[a], n == 0, n == 3)
                n_summed += len(last_panels)
                last_panels = []
                if n_summed == 4:
                    summed.extend((2 * last_q + a, last_acc[a]) for a in range(2))
            for (q, g), banks in zip(panels, products):
                localised.append((s, q, g, localise(q, g, banks)))
        for n, (i, acc) in enumerate(summed):
            store(i, acc, on_vector=(n == 0))
